import numpy as np
import ml_dtypes


def mxq(x, axis, fmt="e4m3"):
    dtype, down = {"e4m3": (ml_dtypes.float8_e4m3fn, 7), "e5m2": (ml_dtypes.float8_e5m2, 14)}[fmt]
    v = np.moveaxis(np.asarray(x, np.float32).astype(ml_dtypes.bfloat16).astype(np.float64), axis, -1)
    blocks = v.reshape(v.shape[:-1] + (-1, 32))
    amax = np.abs(blocks).max(-1, keepdims=True)
    byte = np.maximum(np.where(amax > 0, np.frexp(amax)[1] - 1 + 127, 0) - down, 1)
    scale = np.exp2(byte - 127.0)
    codes = (blocks / scale).astype(np.float32).astype(dtype).astype(np.float64)
    return np.moveaxis((codes * scale).reshape(v.shape), -1, axis)


WIDE = False


def mx_kscale(k):
    if not WIDE:
        return np.ones(k)
    levels = np.array([10, -10, 5, -5, 0])
    if k % 512:
        return np.exp2(np.random.permutation(np.resize(levels, k // 32))).repeat(32)
    a = np.empty((k // 512, 16))
    for p in range(k // 512):
        a[p, :8] = np.random.permutation(np.resize(levels, 8))
        for g in range(8):
            far = levels[np.abs(levels - a[p, g]) >= 10]
            a[p, g + 8] = far[np.random.randint(len(far))]
    return np.exp2(a.ravel()).repeat(32)


def f64(x):
    return np.asarray(x).astype(np.float64)


def striped(idx):
    return np.tile(idx.reshape(-1, 16).T, (8, 1)).astype(np.uint16)


def unstriped(offs):
    return offs[:16].T.reshape(-1).astype(np.int64)


E2M1 = np.array([0.0, 0.5, 1.0, 1.5, 2.0, 3.0, 4.0, 6.0, -0.0, -0.5, -1.0, -1.5, -2.0, -3.0, -4.0, -6.0])


def pack_weight(w, fmt):
    k, n = w.shape
    w = f64(np.asarray(w, np.float32).astype(ml_dtypes.bfloat16)).reshape(k // 32, 32, n)
    amax = np.abs(w).max(1)
    if fmt == "e4m3":
        byte = np.frexp(amax)[1] - 1 + 127 - 7
    else:
        mant, ex = np.frexp(amax / 6.0)
        byte = np.where(mant > 0.5, ex, ex - 1) + 127
    byte = np.clip(np.where(amax > 0, byte, 1), 1, 254)
    scaled = (w * np.exp2(127.0 - byte)[:, None, :]).reshape(k, n).astype(np.float32)
    by_word = np.ascontiguousarray(scaled.reshape(k // 512, 128, 4, n).transpose(0, 1, 3, 2))
    if fmt == "e4m3":
        words = by_word.astype(ml_dtypes.float8_e4m3fn).view(np.uint8)
    else:
        c = by_word.astype(ml_dtypes.float4_e2m1fn).view(np.uint8) & 0xF
        words = (c[..., 0::2] | (c[..., 1::2] << 4)).reshape(k // 512, 128, 2 * n)
    return np.ascontiguousarray(words), np.ascontiguousarray(byte.astype(np.uint8).reshape(k // 512, 16, n))


def unpack_weight(words, scales, fmt):
    g, _, n = scales.shape
    words = np.ascontiguousarray(words).reshape(g, 128, n, -1)
    if fmt == "e4m3":
        vals = words.view(ml_dtypes.float8_e4m3fn).astype(np.float64)
    else:
        nib = np.empty((g, 128, n, 4), np.uint8)
        nib[..., 0::2] = words & 0xF
        nib[..., 1::2] = words >> 4
        vals = E2M1[nib]
    vals = vals * np.repeat(np.exp2(scales.astype(np.float64) - 127.0), 8, axis=1)[..., None]
    return vals.transpose(0, 1, 3, 2).reshape(g * 512, n)


def gelu(v):
    return 0.5 * v * (1.0 + np.tanh(np.sqrt(2.0 / np.pi) * (v + 0.044715 * v**3)))


K, T, S, H, T2, P, T3, S2 = 1024, 2048, 512, 1024, 1024, 512, 2048, 1024

def setup_inputs():
    n = np.random.standard_normal
    s = mx_kscale(K)[:, None]
    u = mx_kscale(H)[:, None]
    tab_words, tab_scales = pack_weight(n((K, T)) * s, "e4m3")
    tab2_words, tab2_scales = pack_weight(n((H, T3)) / np.sqrt(H) / u, "e4m3")
    w4_words, w4_scales = pack_weight(1.5 * n((K, H)) / np.sqrt(K) / s, "e2m1")
    return {
        "tab_words": tab_words, "tab_scales": tab_scales,
        "tab2_words": tab2_words, "tab2_scales": tab2_scales,
        "w1": (0.8 * n((K, H)) / np.sqrt(K) / s).astype(np.float32),
        "w4_words": w4_words, "w4_scales": w4_scales,
        "b4": (0.9 * n(H)).astype(np.float32),
        "sess": (np.exp(0.3 * n((H, S))) * u).astype(np.float32),
        "wgs": np.exp(0.3 * n((128, S))).astype(np.float32),
        "page0": (n((H, T2)) * u).astype(np.float32),
        "cv": np.exp(0.3 * n(S2)).astype(np.float32),
        "offs": striped(np.random.permutation(T)[:S]),
        "offs2": striped(np.random.permutation(T3)[:S2]),
        "offs3": striped(np.random.permutation(T2)[:S]),
        "offs4": striped(np.random.permutation(T2)[:P]),
    }

def reference(tab_words, tab_scales, tab2_words, tab2_scales, w1, w4_words, w4_scales, b4, sess, wgs, page0, cv, offs, offs2, offs3, offs4):
    v = unpack_weight(tab_words, tab_scales, "e4m3")[:, unstriped(offs)]
    v2 = unpack_weight(tab2_words, tab2_scales, "e4m3")[:, unstriped(offs2)]
    a = mxq(f64(w1), 0, "e4m3").T @ v
    b = unpack_weight(w4_words, w4_scales, "e2m1").T @ v
    h = f64(sess) * (a + np.tanh(b + f64(b4)[:, None]))
    page = f64(page0).copy()
    page[:, unstriped(offs3)] = np.tile(f64(wgs), (H // 128, 1)) * h
    x = page[:, unstriped(offs4)]
    e = v2.T @ mxq(np.abs(x), 0, "e4m3")
    d = v2.T @ mxq(x, 0, "e4m3")
    return np.maximum(e, f64(cv)[:, None] * d)

@@ -1,0 +1,299 @@
+from contextlib import ExitStack
+
+import concourse.mybir as mybir
+from concourse.masks import make_identity
+
+K, T, S, H, T2, NP, T3, S2 = 1024, 2048, 512, 1024, 1024, 512, 2048, 1024
+FLOPS = 2 * (2 * K * H * S + 2 * H * S2 * NP)
+
+F32 = mybir.dt.float32
+BF16 = mybir.dt.bfloat16
+I32 = mybir.dt.int32
+U32 = mybir.dt.uint32
+U16 = mybir.dt.uint16
+U8 = mybir.dt.uint8
+FP8X4 = mybir.dt.float8_e4m3fn_x4
+FP4X4 = mybir.dt.float4_e2m1fn_x4
+ALU = mybir.AluOpType
+ACT = mybir.ActivationFunctionType
+
+P = 128
+PACK = 4
+KP = P * PACK
+
+
+def tile_list_manual_help_scores_kernel(
+    tc, tab_words, tab_scales, tab2_words, tab2_scales, w1, w4_words, w4_scales, b4, sess, wgs, page0, cv,
+    offs, offs2, offs3, offs4, out,
+):
+    nc = tc.nc
+    with ExitStack() as ctx:
+        keep = ctx.enter_context(tc.tile_pool(name="keep", bufs=1))
+        ring = ctx.enter_context(tc.tile_pool(name="ring", bufs=4))
+        psum = ctx.enter_context(tc.psum_pool(name="psum", bufs=1))
+
+        def held(shape, dtype, name):
+            return keep.tile(shape, dtype, name=name, align_bytes=64)
+
+        def bank(n):
+            return psum.tile([P, 512], F32, name="bank%d" % n)
+
+        def load_list(src, entries, name):
+            dst = keep.tile([P, entries // 16], U16, name=name)
+            nc.sync.dma_start(dst[:], src)
+            return dst
+
+        def load_words(src, a, name):
+            dst = held([P, src.shape[2]], U32, name)
+            nc.sync.dma_start(dst[:].bitcast(I32), src[a].rearrange("p t i -> p (t i)").bitcast(I32))
+            return dst
+
+        def zeroed_bytes(width, name):
+            dst = held([P, width], U8, name)
+            nc.vector.memset(dst[:].bitcast(I32), 0)
+            return dst
+
+        def load_scale_rows(queue, dst, src):
+            for q in range(4):
+                queue.dma_start(dst[32 * q : 32 * q + 8, :].bitcast(I32), src[:, 4 * q : 4 * q + 4, :].bitcast(I32))
+
+        def load_scale_planes(queue, dst, src):
+            for r in range(4):
+                queue.dma_start(
+                    dst[r:P:32, :].bitcast(I32).rearrange("q (a c) -> q a c", a=2),
+                    src.bitcast(I32).rearrange("a (q r) c -> r q a c", r=4)[r],
+                )
+
+        def load_w1(a, b):
+            dst = ring.tile([P, PACK, KP], F32, name="wide")
+            nc.sync.dma_start(dst[:], w1[KP * a : KP * (a + 1), KP * b : KP * (b + 1)].rearrange("(p i) c -> p i c", i=PACK))
+            return dst
+
+        def load_w4(b):
+            dst = held([P, 2, KP], U16, "w4raw%d" % b)
+            nc.sync.dma_start(
+                dst[:].bitcast(I32), w4_words[:, :, 2 * KP * b : 2 * KP * (b + 1)].rearrange("a p c -> p a c").bitcast(I32)
+            )
+            return dst
+
+        def load_wgs(t0, t1):
+            dst = held([P, t1 - t0, S], F32, "wgs%d" % t0)
+            rows = wgs.rearrange("(q t) j -> q t j", t=PACK)[:, t0:t1, :]
+            for q in range(4):
+                nc.sync.dma_start(dst[32 * q : 32 * (q + 1), :, :], rows)
+            return [dst[:, t, :] for t in range(t1 - t0)]
+
+        def load_rows(src, s, name):
+            b, t = divmod(s, PACK)
+            dst = held([P, src.shape[1]], F32, "%s%d" % (name, s))
+            nc.sync.dma_start(dst[:], src[KP * b : KP * (b + 1), :].rearrange("(p t) j -> t p j", t=PACK)[t])
+            return dst
+
+        tab_sc = zeroed_bytes(2 * T, "tab_sc")
+        w4_sc = zeroed_bytes(2 * H, "w4_sc")
+        tab2_sc = zeroed_bytes(T3, "tab2_sc")
+
+        tabw = [load_words(tab_words, 0, "tabw0")]
+        idx = load_list(offs, S, "idx")
+        idx2 = load_list(offs2, S2, "idx2")
+        idx3 = load_list(offs3, S, "idx3")
+        idx4 = load_list(offs4, NP, "idx4")
+        b4_col = held([P, 2, PACK], F32, "b4_col")
+        nc.sync.dma_start(b4_col[:], b4.rearrange("(b p t) -> p b t", b=2, t=PACK))
+        w4raw = [load_w4(0)]
+        w1raw = {(0, 0): load_w1(0, 0)}
+        load_scale_planes(nc.gpsimd, tab_sc, tab_scales)
+        load_scale_planes(nc.gpsimd, w4_sc, w4_scales)
+        w1raw[(1, 0)] = load_w1(1, 0)
+        tabw.append(load_words(tab_words, 1, "tabw1"))
+        sess_sb = [load_rows(sess, 0, "sess")]
+        wgs_sb = load_wgs(0, 1)
+        page = [load_rows(page0, 0, "page")]
+        sess_sb.append(load_rows(sess, 1, "sess"))
+        wgs_sb = wgs_sb + load_wgs(1, PACK)
+        w4raw.append(load_w4(1))
+        page.append(load_rows(page0, 1, "page"))
+        load_scale_rows(nc.sync, tab2_sc, tab2_scales)
+        w1raw[(0, 1)] = load_w1(0, 1)
+        sess_sb.append(load_rows(sess, 2, "sess"))
+        page.append(load_rows(page0, 2, "page"))
+        w1raw[(1, 1)] = load_w1(1, 1)
+        sess_sb.append(load_rows(sess, 3, "sess"))
+        page.append(load_rows(page0, 3, "page"))
+        for s in (4, 5):
+            sess_sb.append(load_rows(sess, s, "sess"))
+            page.append(load_rows(page0, s, "page"))
+        tab2w = [load_words(tab2_words, a, "tab2w%d" % a) for a in range(2)]
+        for s in (6, 7):
+            sess_sb.append(load_rows(sess, s, "sess"))
+            page.append(load_rows(page0, s, "page"))
+        cv_col = held([P, S2 // P], F32, "cv_col")
+        with nc.allow_non_contiguous_dma(reason="one factor a partition"):
+            nc.sync.dma_start(cv_col[:], cv.rearrange("(c p) -> p c", p=P))
+
+        v_w = [held([P, S], U32, "v_w%d" % a) for a in range(2)]
+        v_sc = [held([P, S], U8, "v_sc%d" % a) for a in range(2)]
+        ident = held([P, P], F32, "ident")
+        make_identity(nc, ident[:])
+
+        w1_q, w1_sc, w4_w, w4_scp = {}, {}, {}, {}
+
+        def prepare_w1(a, b, slot, codes):
+            rounded = held([P, PACK * KP], BF16, slot)
+            nc.scalar.copy(
+                rounded[:].rearrange("p (t m i) -> p m t i", t=PACK, i=PACK),
+                w1raw[(a, b)][:].rearrange("p i (m t) -> p m t i", t=PACK),
+            )
+            w1_q[(a, b)] = codes
+            w1_sc[(a, b)] = held([P, KP], U8, "w1_sc%d%d" % (a, b))
+            nc.vector.quantize_mx(codes.bitcast(FP8X4), w1_sc[(a, b)][:], rounded[:])
+
+        def deal_w4_words(b, slot):
+            w4_w[b] = held([P, 2, KP], U16, slot)
+            nc.vector.tensor_copy(
+                w4_w[b][:].rearrange("p a (t m) -> p a t m", t=PACK), w4raw[b][:].rearrange("p a (m t) -> p a t m", t=PACK)
+            )
+
+        def deal_w4_scales(b, scale_slot):
+            w4_scp[b] = held([P, 2, KP], U8, scale_slot)
+            nc.vector.tensor_copy(
+                w4_scp[b][:].rearrange("p a (t m) -> p a t m", t=PACK),
+                w4_sc[:].rearrange("p (a b m t) -> p b a t m", a=2, b=2, t=PACK)[:, b],
+            )
+
+        nc.vector.tensor_copy(v_w[0][:], tabw[0][:].indirect(idx[:]))
+        deal_w4_words(0, "w4_w0")
+        for a in range(2):
+            nc.vector.tensor_copy(v_sc[a][:], tab_sc[:, T * a : T * (a + 1)].indirect(idx[:]))
+        w1_codes = held([P, 2, KP], U32, "w1_codes")
+        prepare_w1(0, 0, "x_signed", w1_codes[:, 0, :])
+        deal_w4_scales(0, "w4_scp0")
+        prepare_w1(1, 0, "x_abs", w1_codes[:, 1, :])
+        nc.vector.tensor_copy(v_w[1][:], tabw[1][:].indirect(idx[:]))
+
+        picked = {}
+        x_q, x_sc = {}, {}
+
+        def first_stage(s):
+            b, t = divmod(s, PACK)
+            cols = slice(P * t, P * (t + 1))
+            acc_b, acc_a = bank(4 * (s % 2)), bank(4 * (s % 2) + 1)
+            for a in range(2):
+                nc.tensor.matmul_mx(
+                    acc_b[:], lhsT=w4_w[b][:, a, cols].bitcast(FP4X4), lhsT_scale=w4_scp[b][:, a, cols],
+                    rhs=v_w[a][:].bitcast(FP8X4), rhs_scale=v_sc[a][:], start=(a == 0), stop=(a == 1),
+                )
+            for a in range(2):
+                nc.tensor.matmul_mx(
+                    acc_a[:], lhsT=w1_q[(a, b)][:, cols].bitcast(FP8X4), lhsT_scale=w1_sc[(a, b)][:, cols],
+                    rhs=v_w[a][:].bitcast(FP8X4), rhs_scale=v_sc[a][:], start=(a == 0), stop=(a == 1),
+                )
+            gate = ring.tile([P, S], F32, name="gate", bufs=2)
+            nc.scalar.activation(gate[:], acc_b[:], ACT.Tanh, bias=b4_col[:, b, t : t + 1])
+            factor = ring.tile([P, S], F32, name="factor", bufs=1)
+            nc.vector.tensor_tensor(factor[:], sess_sb[s][:], wgs_sb[t], ALU.mult)
+            total = ring.tile([P, S], F32, name="total", bufs=3)
+            if s == 0:
+                nc.vector.tensor_tensor(total[:], acc_a[:], gate[:], ALU.add)
+                return total, factor
+            linear = ring.tile([P, S], F32, name="linear", bufs=2)
+            nc.scalar.copy(linear[:], acc_a[:])
+            sum_t = bank(2)
+            for c in range(4):
+                blk = slice(P * c, P * (c + 1))
+                nc.tensor.matmul(sum_t[:, blk], lhsT=gate[:, blk], rhs=ident[:], start=True, stop=False, is_transpose=True)
+                nc.tensor.matmul(sum_t[:, blk], lhsT=linear[:, blk], rhs=ident[:], start=False, stop=True, is_transpose=True)
+            turned = held([P, S], F32, "turned%d" % s)
+            nc.scalar.copy(turned[:], sum_t[:])
+            back = bank(3)
+            for c in range(4):
+                blk = slice(P * c, P * (c + 1))
+                nc.tensor.transpose(back[:, blk], turned[:, blk], ident[:])
+            nc.scalar.copy(total[:], back[:])
+            return total, factor
+
+        def rewrite(s, total):
+            nc.vector.tensor_tensor(page[s][:].indirect(idx3[:]), total[0][:], total[1][:], ALU.mult)
+
+        def pick(s):
+            b, t = divmod(s, PACK)
+            if t == 0:
+                picked[b] = ring.tile([P, PACK, NP], F32, name="wide")
+            nc.vector.tensor_copy(picked[b][:, t, :], page[s][:].indirect(idx4[:]))
+
+        def round_x(b, slots):
+            src = picked[b][:].rearrange("p t j -> p j t")
+            signed = held([P, PACK * NP], BF16, slots[0])
+            nc.scalar.copy(signed[:].rearrange("p (j t) -> p j t", t=PACK), src)
+            absolute = held([P, PACK * NP], BF16, slots[1])
+            nc.scalar.activation(absolute[:].rearrange("p (j t) -> p j t", t=PACK), src, ACT.Abs)
+            return signed, absolute
+
+        def quantize_x(b, pair, slot):
+            codes = held([P, 2, NP], U32, slot)
+            for n in range(2):
+                x_q[(b, n)] = codes[:, n, :]
+                x_sc[(b, n)] = held([P, NP], U8, "x_sc%d%d" % (b, n))
+                nc.vector.quantize_mx(x_q[(b, n)].bitcast(FP8X4), x_sc[(b, n)][:], pair[n][:])
+
+        v2_w = {}
+
+        def gather_v2(a, half, slot):
+            v2_w[(a, half)] = held([P, S2 // 2], U32, slot)
+            nc.vector.tensor_copy(v2_w[(a, half)][:], tab2w[a][:].indirect(idx2[:, 32 * half : 32 * (half + 1)]))
+
+        def score_pass(acc, m, n, b):
+            half, c = divmod(m, 4)
+            nc.tensor.matmul_mx(
+                acc[:], lhsT=v2_w[(b, half)][:, P * c : P * (c + 1)].bitcast(FP8X4), lhsT_scale=v2_sc[4 * b : P, P * m : P * (m + 1)],
+                rhs=x_q[(b, n)].bitcast(FP8X4), rhs_scale=x_sc[(b, n)][:], start=(b == 0), stop=(b == 1),
+            )
+
+        def finish(m, acc_d, acc_e):
+            res = ring.tile([P, NP], F32, name="res")
+            nc.scalar.activation(res[:], acc_d[:], ACT.Copy, scale=cv_col[:, m : m + 1])
+            nc.vector.tensor_tensor(res[:], acc_e[:], res[:], ALU.max)
+            nc.sync.dma_start(out[P * m : P * (m + 1), :], res[:])
+
+        total = first_stage(0)
+        deal_w4_scales(1, "w4_scp1")
+        for s in range(8):
+            rewrite(s, total)
+            if s + 1 < 8:
+                total = first_stage(s + 1)
+            pick(s)
+            if s == 0:
+                deal_w4_words(1, "sess1")
+            if s == 1:
+                w1_codes = held([P, 2, KP], U32, "page1")
+                prepare_w1(0, 1, "turned1", w1_codes[:, 0, :])
+                prepare_w1(1, 1, "turned2", w1_codes[:, 1, :])
+            if s == 2:
+                v2_sc = held([P, S2], U8, "page2")
+                nc.vector.tensor_copy(v2_sc[:], tab2_sc[:].indirect(idx2[:]))
+            if s == 4:
+                gather_v2(0, 0, "page4")
+            if s == 5:
+                gather_v2(1, 0, "page5")
+        pair0 = round_x(0, ("turned6", "turned7"))
+        quantize_x(0, pair0, "page7")
+        accs = {}
+        for m in range(4):
+            accs[m] = (bank((2 * m + 4) % 8), bank((2 * m + 5) % 8))
+        for n in range(2):
+            for m in range(4):
+                score_pass(accs[m][n], m, n, 0)
+        pair1 = round_x(1, ("x_signed", "x_abs"))
+        gather_v2(0, 1, "turned6")
+        quantize_x(1, pair1, "x_codes")
+        gather_v2(1, 1, "x_signed")
+        for n in range(2):
+            for m in range(4):
+                score_pass(accs[m][n], m, n, 1)
+        for m in range(8):
+            if m >= 4:
+                accs[m] = (bank((2 * m + 4) % 8), bank((2 * m + 5) % 8))
+                for n in range(2):
+                    for b in range(2):
+                        score_pass(accs[m][n], m, n, b)
+            finish(m, accs[m][0], accs[m][1])

@@ -48,9 +48,9 @@ def tile_list_manual_help_scores_kernel(
             nc.sync.dma_start(dst[:].bitcast(I32), src[a].rearrange("p t i -> p (t i)").bitcast(I32))
             return dst
 
-        def zeroed_bytes(width, name):
+        def zeroed_bytes(engine, width, name):
             dst = held([P, width], U8, name)
-            nc.vector.memset(dst[:].bitcast(I32), 0)
+            engine.memset(dst[:].bitcast(I32), 0)
             return dst
 
         def load_scale_rows(queue, dst, src):
@@ -69,13 +69,6 @@ def tile_list_manual_help_scores_kernel(
             nc.sync.dma_start(dst[:], w1[KP * a : KP * (a + 1), KP * b : KP * (b + 1)].rearrange("(p i) c -> p i c", i=PACK))
             return dst
 
-        def load_w4(b):
-            dst = held([P, 2, KP], U16, "w4raw%d" % b)
-            nc.sync.dma_start(
-                dst[:].bitcast(I32), w4_words[:, :, 2 * KP * b : 2 * KP * (b + 1)].rearrange("a p c -> p a c").bitcast(I32)
-            )
-            return dst
-
         def load_wgs(t0, t1):
             dst = held([P, t1 - t0, S], F32, "wgs%d" % t0)
             rows = wgs.rearrange("(q t) j -> q t j", t=PACK)[:, t0:t1, :]
@@ -89,44 +82,38 @@ def tile_list_manual_help_scores_kernel(
             nc.sync.dma_start(dst[:], src[KP * b : KP * (b + 1), :].rearrange("(p t) j -> t p j", t=PACK)[t])
             return dst
 
-        tab_sc = zeroed_bytes(2 * T, "tab_sc")
-        w4_sc = zeroed_bytes(2 * H, "w4_sc")
-        tab2_sc = zeroed_bytes(T3, "tab2_sc")
+        tab_sc = zeroed_bytes(nc.vector, 2 * T, "tab_sc")
+        w4_sc = zeroed_bytes(nc.vector, 2 * H, "w4_sc")
+        tab2_sc = zeroed_bytes(nc.gpsimd, T3, "tab2_sc")
 
         tabw = [load_words(tab_words, 0, "tabw0")]
         idx = load_list(offs, S, "idx")
         idx2 = load_list(offs2, S2, "idx2")
-        idx3 = load_list(offs3, S, "idx3")
-        idx4 = load_list(offs4, NP, "idx4")
-        b4_col = held([P, 2, PACK], F32, "b4_col")
-        nc.sync.dma_start(b4_col[:], b4.rearrange("(b p t) -> p b t", b=2, t=PACK))
-        w4raw = [load_w4(0)]
+        w4raw = held([P, 2, H], U16, "w4raw")
+        nc.sync.dma_start(w4raw[:].bitcast(I32), w4_words.rearrange("a p c -> p a c").bitcast(I32))
+        tab2w = [load_words(tab2_words, 0, "tab2w0")]
         w1raw = {(0, 0): load_w1(0, 0)}
         load_scale_planes(nc.gpsimd, tab_sc, tab_scales)
         load_scale_planes(nc.gpsimd, w4_sc, w4_scales)
-        w1raw[(1, 0)] = load_w1(1, 0)
+        b4_col = held([P, 2, PACK], F32, "b4_col")
+        nc.sync.dma_start(b4_col[:], b4.rearrange("(b p t) -> p b t", b=2, t=PACK))
         tabw.append(load_words(tab_words, 1, "tabw1"))
+        w1raw[(1, 0)] = load_w1(1, 0)
+        load_scale_rows(nc.sync, tab2_sc, tab2_scales)
+        idx3 = load_list(offs3, S, "idx3")
+        idx4 = load_list(offs4, NP, "idx4")
         sess_sb = [load_rows(sess, 0, "sess")]
         wgs_sb = load_wgs(0, 1)
         page = [load_rows(page0, 0, "page")]
+        w1raw[(0, 1)] = load_w1(0, 1)
         sess_sb.append(load_rows(sess, 1, "sess"))
         wgs_sb = wgs_sb + load_wgs(1, PACK)
-        w4raw.append(load_w4(1))
         page.append(load_rows(page0, 1, "page"))
-        load_scale_rows(nc.sync, tab2_sc, tab2_scales)
-        w1raw[(0, 1)] = load_w1(0, 1)
-        sess_sb.append(load_rows(sess, 2, "sess"))
-        page.append(load_rows(page0, 2, "page"))
         w1raw[(1, 1)] = load_w1(1, 1)
-        sess_sb.append(load_rows(sess, 3, "sess"))
-        page.append(load_rows(page0, 3, "page"))
-        for s in (4, 5):
+        for s in range(2, 8):
             sess_sb.append(load_rows(sess, s, "sess"))
             page.append(load_rows(page0, s, "page"))
-        tab2w = [load_words(tab2_words, a, "tab2w%d" % a) for a in range(2)]
-        for s in (6, 7):
-            sess_sb.append(load_rows(sess, s, "sess"))
-            page.append(load_rows(page0, s, "page"))
+        tab2w.append(load_words(tab2_words, 1, "tab2w1"))
         cv_col = held([P, S2 // P], F32, "cv_col")
         with nc.allow_non_contiguous_dma(reason="one factor a partition"):
             nc.sync.dma_start(cv_col[:], cv.rearrange("(c p) -> p c", p=P))
@@ -136,7 +123,11 @@ def tile_list_manual_help_scores_kernel(
         ident = held([P, P], F32, "ident")
         make_identity(nc, ident[:])
 
-        w1_q, w1_sc, w4_w, w4_scp = {}, {}, {}, {}
+        w1_q, w1_sc, v2_w = {}, {}, {}
+
+        def gather_v2(a, half, slot):
+            v2_w[(a, half)] = held([P, S2 // 2], U32, slot)
+            nc.vector.tensor_copy(v2_w[(a, half)][:], tab2w[a][:].indirect(idx2[:, 32 * half : 32 * (half + 1)]))
 
         def prepare_w1(a, b, slot, codes):
             rounded = held([P, PACK * KP], BF16, slot)
@@ -148,28 +139,28 @@ def tile_list_manual_help_scores_kernel(
             w1_sc[(a, b)] = held([P, KP], U8, "w1_sc%d%d" % (a, b))
             nc.vector.quantize_mx(codes.bitcast(FP8X4), w1_sc[(a, b)][:], rounded[:])
 
-        def deal_w4_words(b, slot):
-            w4_w[b] = held([P, 2, KP], U16, slot)
+        def deal(src, b, dtype, name):
+            dst = held([P, 2, KP], dtype, name)
             nc.vector.tensor_copy(
-                w4_w[b][:].rearrange("p a (t m) -> p a t m", t=PACK), w4raw[b][:].rearrange("p a (m t) -> p a t m", t=PACK)
+                dst[:].rearrange("p a (t m) -> p a t m", t=PACK),
+                src[:, :, KP * b : KP * (b + 1)].rearrange("p a (m t) -> p a t m", t=PACK),
             )
-
-        def deal_w4_scales(b, scale_slot):
-            w4_scp[b] = held([P, 2, KP], U8, scale_slot)
-            nc.vector.tensor_copy(
-                w4_scp[b][:].rearrange("p a (t m) -> p a t m", t=PACK),
-                w4_sc[:].rearrange("p (a b m t) -> p b a t m", a=2, b=2, t=PACK)[:, b],
-            )
+            return dst
 
         nc.vector.tensor_copy(v_w[0][:], tabw[0][:].indirect(idx[:]))
-        deal_w4_words(0, "w4_w0")
+        w4_w = [deal(w4raw, b, U16, "w4_w%d" % b) for b in range(2)]
+        gather_v2(0, 0, "v2_w00")
+        gather_v2(0, 1, "v2_w01")
         for a in range(2):
             nc.vector.tensor_copy(v_sc[a][:], tab_sc[:, T * a : T * (a + 1)].indirect(idx[:]))
+        nc.vector.tensor_copy(v_w[1][:], tabw[1][:].indirect(idx[:]))
         w1_codes = held([P, 2, KP], U32, "w1_codes")
         prepare_w1(0, 0, "x_signed", w1_codes[:, 0, :])
-        deal_w4_scales(0, "w4_scp0")
+        w4_planes = w4_sc[:].rearrange("p (a c) -> p a c", a=2)
+        w4_scp = [deal(w4_planes, 0, U8, "w4_scp0")]
+        v2_sc = held([P, S2], U8, "v2_sc")
+        nc.vector.tensor_copy(v2_sc[:], tab2_sc[:].indirect(idx2[:]))
         prepare_w1(1, 0, "x_abs", w1_codes[:, 1, :])
-        nc.vector.tensor_copy(v_w[1][:], tabw[1][:].indirect(idx[:]))
 
         picked = {}
         x_q, x_sc = {}, {}
@@ -188,12 +179,12 @@ def tile_list_manual_help_scores_kernel(
                     acc_a[:], lhsT=w1_q[(a, b)][:, cols].bitcast(FP8X4), lhsT_scale=w1_sc[(a, b)][:, cols],
                     rhs=v_w[a][:].bitcast(FP8X4), rhs_scale=v_sc[a][:], start=(a == 0), stop=(a == 1),
                 )
-            gate = ring.tile([P, S], F32, name="gate", bufs=2)
+            gate = held([P, S], F32, "gate%d" % (s if s < 2 else 2 + s % 2))
             nc.scalar.activation(gate[:], acc_b[:], ACT.Tanh, bias=b4_col[:, b, t : t + 1])
             factor = ring.tile([P, S], F32, name="factor", bufs=1)
             nc.vector.tensor_tensor(factor[:], sess_sb[s][:], wgs_sb[t], ALU.mult)
             total = ring.tile([P, S], F32, name="total", bufs=3)
-            if s == 0:
+            if s < 2:
                 nc.vector.tensor_tensor(total[:], acc_a[:], gate[:], ALU.add)
                 return total, factor
             linear = ring.tile([P, S], F32, name="linear", bufs=2)
@@ -221,79 +212,82 @@ def tile_list_manual_help_scores_kernel(
                 picked[b] = ring.tile([P, PACK, NP], F32, name="wide")
             nc.vector.tensor_copy(picked[b][:, t, :], page[s][:].indirect(idx4[:]))
 
-        def round_x(b, slots):
-            src = picked[b][:].rearrange("p t j -> p j t")
-            signed = held([P, PACK * NP], BF16, slots[0])
-            nc.scalar.copy(signed[:].rearrange("p (j t) -> p j t", t=PACK), src)
-            absolute = held([P, PACK * NP], BF16, slots[1])
-            nc.scalar.activation(absolute[:].rearrange("p (j t) -> p j t", t=PACK), src, ACT.Abs)
-            return signed, absolute
+        def round_x(dst, b, n, t0, t1):
+            src = picked[b][:, t0:t1, :].rearrange("p t j -> p j t")
+            view = dst[:].rearrange("p (j t) -> p j t", t=PACK)[:, :, t0:t1]
+            if n == 0:
+                nc.scalar.copy(view, src)
+            else:
+                nc.scalar.activation(view, src, ACT.Abs)
 
-        def quantize_x(b, pair, slot):
-            codes = held([P, 2, NP], U32, slot)
-            for n in range(2):
-                x_q[(b, n)] = codes[:, n, :]
-                x_sc[(b, n)] = held([P, NP], U8, "x_sc%d%d" % (b, n))
-                nc.vector.quantize_mx(x_q[(b, n)].bitcast(FP8X4), x_sc[(b, n)][:], pair[n][:])
-
-        v2_w = {}
-
-        def gather_v2(a, half, slot):
-            v2_w[(a, half)] = held([P, S2 // 2], U32, slot)
-            nc.vector.tensor_copy(v2_w[(a, half)][:], tab2w[a][:].indirect(idx2[:, 32 * half : 32 * (half + 1)]))
+        def quantize_x(b, n, rounded, slot):
+            x_q[(b, n)] = held([P, NP], U32, slot)
+            x_sc[(b, n)] = held([P, NP], U8, "x_sc%d%d" % (b, n))
+            nc.vector.quantize_mx(x_q[(b, n)][:].bitcast(FP8X4), x_sc[(b, n)][:], rounded[:])
 
         def score_pass(acc, m, n, b):
             half, c = divmod(m, 4)
             nc.tensor.matmul_mx(
                 acc[:], lhsT=v2_w[(b, half)][:, P * c : P * (c + 1)].bitcast(FP8X4), lhsT_scale=v2_sc[4 * b : P, P * m : P * (m + 1)],
-                rhs=x_q[(b, n)].bitcast(FP8X4), rhs_scale=x_sc[(b, n)][:], start=(b == 0), stop=(b == 1),
+                rhs=x_q[(b, n)][:].bitcast(FP8X4), rhs_scale=x_sc[(b, n)][:], start=(b == 0), stop=(b == 1),
             )
 
-        def finish(m, acc_d, acc_e):
-            res = ring.tile([P, NP], F32, name="res")
+        def scale_d(m, acc_d):
+            res = ring.tile([P, NP], F32, name="res", bufs=8)
             nc.scalar.activation(res[:], acc_d[:], ACT.Copy, scale=cv_col[:, m : m + 1])
+            return res
+
+        def finish(m, res, acc_e):
             nc.vector.tensor_tensor(res[:], acc_e[:], res[:], ALU.max)
             nc.sync.dma_start(out[P * m : P * (m + 1), :], res[:])
 
         total = first_stage(0)
-        deal_w4_scales(1, "w4_scp1")
+        w4_scp.append(deal(w4_planes, 1, U8, "w4_scp1"))
         for s in range(8):
             rewrite(s, total)
             if s + 1 < 8:
                 total = first_stage(s + 1)
             pick(s)
-            if s == 0:
-                deal_w4_words(1, "sess1")
             if s == 1:
                 w1_codes = held([P, 2, KP], U32, "page1")
-                prepare_w1(0, 1, "turned1", w1_codes[:, 0, :])
-                prepare_w1(1, 1, "turned2", w1_codes[:, 1, :])
-            if s == 2:
-                v2_sc = held([P, S2], U8, "page2")
-                nc.vector.tensor_copy(v2_sc[:], tab2_sc[:].indirect(idx2[:]))
-            if s == 4:
-                gather_v2(0, 0, "page4")
-            if s == 5:
-                gather_v2(1, 0, "page5")
-        pair0 = round_x(0, ("turned6", "turned7"))
-        quantize_x(0, pair0, "page7")
+                prepare_w1(0, 1, "gate0", w1_codes[:, 0, :])
+                prepare_w1(1, 1, "gate1", w1_codes[:, 1, :])
+            if s == 6:
+                first = [held([P, PACK * NP], BF16, "turned%d" % (5 + n)) for n in range(2)]
+                for n in range(2):
+                    round_x(first[n], 0, n, 0, PACK)
+                quantize_x(0, 0, first[0], "page6")
+                second = [held([P, PACK * NP], BF16, name) for name in ("turned7", "turned5")]
+                for n in range(2):
+                    round_x(second[n], 1, n, 0, 2)
+        quantize_x(0, 1, first[1], "page7")
         accs = {}
         for m in range(4):
             accs[m] = (bank((2 * m + 4) % 8), bank((2 * m + 5) % 8))
         for n in range(2):
             for m in range(4):
                 score_pass(accs[m][n], m, n, 0)
-        pair1 = round_x(1, ("x_signed", "x_abs"))
-        gather_v2(0, 1, "turned6")
-        quantize_x(1, pair1, "x_codes")
-        gather_v2(1, 1, "x_signed")
+        for n in range(2):
+            round_x(second[n], 1, n, 2, PACK)
+        gather_v2(1, 0, "turned6")
+        quantize_x(1, 0, second[0], "x_signed")
+        gather_v2(1, 1, "turned7")
+        quantize_x(1, 1, second[1], "x_abs")
         for n in range(2):
             for m in range(4):
                 score_pass(accs[m][n], m, n, 1)
-        for m in range(8):
-            if m >= 4:
-                accs[m] = (bank((2 * m + 4) % 8), bank((2 * m + 5) % 8))
-                for n in range(2):
-                    for b in range(2):
-                        score_pass(accs[m][n], m, n, b)
-            finish(m, accs[m][0], accs[m][1])
+
+        def score_tile(m, n):
+            acc = bank((2 * m + 4 + n) % 8)
+            for b in range(2):
+                score_pass(acc, m, n, b)
+            return acc
+
+        scaled = {m: scale_d(m, accs[m][0]) for m in range(4)}
+        for m in range(4):
+            finish(m, scaled[m], accs[m][1])
+        scaled[4] = scale_d(4, score_tile(4, 0))
+        for m in range(4, 8):
+            if m + 1 < 8:
+                scaled[m + 1] = scale_d(m + 1, score_tile(m + 1, 0))
+            finish(m, scaled[m], score_tile(m, 1))

@@ -69,6 +69,13 @@ def tile_list_manual_help_scores_kernel(
             nc.sync.dma_start(dst[:], w1[KP * a : KP * (a + 1), KP * b : KP * (b + 1)].rearrange("(p i) c -> p i c", i=PACK))
             return dst
 
+        def load_w4(b):
+            dst = held([P, 2, KP], U16, "w4raw%d" % b)
+            nc.sync.dma_start(
+                dst[:].bitcast(I32), w4_words[:, :, 2 * KP * b : 2 * KP * (b + 1)].rearrange("a p c -> p a c").bitcast(I32)
+            )
+            return dst
+
         def load_wgs(t0, t1):
             dst = held([P, t1 - t0, S], F32, "wgs%d" % t0)
             rows = wgs.rearrange("(q t) j -> q t j", t=PACK)[:, t0:t1, :]
@@ -86,11 +93,11 @@ def tile_list_manual_help_scores_kernel(
         w4_sc = zeroed_bytes(nc.vector, 2 * H, "w4_sc")
         tab2_sc = zeroed_bytes(nc.gpsimd, T3, "tab2_sc")
 
-        tabw = [load_words(tab_words, 0, "tabw0")]
+        w4raw = [load_w4(0)]
         idx = load_list(offs, S, "idx")
+        tabw = [load_words(tab_words, 0, "tabw0")]
+        w4raw.append(load_w4(1))
         idx2 = load_list(offs2, S2, "idx2")
-        w4raw = held([P, 2, H], U16, "w4raw")
-        nc.sync.dma_start(w4raw[:].bitcast(I32), w4_words.rearrange("a p c -> p a c").bitcast(I32))
         tab2w = [load_words(tab2_words, 0, "tab2w0")]
         w1raw = {(0, 0): load_w1(0, 0)}
         load_scale_planes(nc.gpsimd, tab_sc, tab_scales)
@@ -98,13 +105,13 @@ def tile_list_manual_help_scores_kernel(
         b4_col = held([P, 2, PACK], F32, "b4_col")
         nc.sync.dma_start(b4_col[:], b4.rearrange("(b p t) -> p b t", b=2, t=PACK))
         tabw.append(load_words(tab_words, 1, "tabw1"))
-        w1raw[(1, 0)] = load_w1(1, 0)
         load_scale_rows(nc.sync, tab2_sc, tab2_scales)
+        w1raw[(1, 0)] = load_w1(1, 0)
         idx3 = load_list(offs3, S, "idx3")
-        idx4 = load_list(offs4, NP, "idx4")
         sess_sb = [load_rows(sess, 0, "sess")]
         wgs_sb = load_wgs(0, 1)
         page = [load_rows(page0, 0, "page")]
+        idx4 = load_list(offs4, NP, "idx4")
         w1raw[(0, 1)] = load_w1(0, 1)
         sess_sb.append(load_rows(sess, 1, "sess"))
         wgs_sb = wgs_sb + load_wgs(1, PACK)
@@ -139,25 +146,28 @@ def tile_list_manual_help_scores_kernel(
             w1_sc[(a, b)] = held([P, KP], U8, "w1_sc%d%d" % (a, b))
             nc.vector.quantize_mx(codes.bitcast(FP8X4), w1_sc[(a, b)][:], rounded[:])
 
-        def deal(src, b, dtype, name):
+        def deal(src, dtype, name):
             dst = held([P, 2, KP], dtype, name)
             nc.vector.tensor_copy(
                 dst[:].rearrange("p a (t m) -> p a t m", t=PACK),
-                src[:, :, KP * b : KP * (b + 1)].rearrange("p a (m t) -> p a t m", t=PACK),
+                src.rearrange("p a (m t) -> p a t m", t=PACK),
             )
             return dst
 
+        w4_w = [deal(w4raw[0][:], U16, "w4_w0")]
         nc.vector.tensor_copy(v_w[0][:], tabw[0][:].indirect(idx[:]))
-        w4_w = [deal(w4raw, b, U16, "w4_w%d" % b) for b in range(2)]
-        gather_v2(0, 0, "v2_w00")
-        gather_v2(0, 1, "v2_w01")
+        w4_w.append(deal(w4raw[1][:], U16, "w4_w1"))
+        v2_first = held([P, S2], U32, "v2_first")
+        nc.vector.tensor_copy(v2_first[:], tab2w[0][:].indirect(idx2[:]))
+        for half in range(2):
+            v2_w[(0, half)] = v2_first[:, S2 // 2 * half : S2 // 2 * (half + 1)]
         for a in range(2):
             nc.vector.tensor_copy(v_sc[a][:], tab_sc[:, T * a : T * (a + 1)].indirect(idx[:]))
         nc.vector.tensor_copy(v_w[1][:], tabw[1][:].indirect(idx[:]))
         w1_codes = held([P, 2, KP], U32, "w1_codes")
         prepare_w1(0, 0, "x_signed", w1_codes[:, 0, :])
         w4_planes = w4_sc[:].rearrange("p (a c) -> p a c", a=2)
-        w4_scp = [deal(w4_planes, 0, U8, "w4_scp0")]
+        w4_scp = [deal(w4_planes[:, :, 0:KP], U8, "w4_scp0")]
         v2_sc = held([P, S2], U8, "v2_sc")
         nc.vector.tensor_copy(v2_sc[:], tab2_sc[:].indirect(idx2[:]))
         prepare_w1(1, 0, "x_abs", w1_codes[:, 1, :])
@@ -181,8 +191,8 @@ def tile_list_manual_help_scores_kernel(
                 )
             gate = held([P, S], F32, "gate%d" % (s if s < 2 else 2 + s % 2))
             nc.scalar.activation(gate[:], acc_b[:], ACT.Tanh, bias=b4_col[:, b, t : t + 1])
-            factor = ring.tile([P, S], F32, name="factor", bufs=1)
-            nc.vector.tensor_tensor(factor[:], sess_sb[s][:], wgs_sb[t], ALU.mult)
+            factor = ring.tile([P, S], F32, name="factor", bufs=2)
+            nc.gpsimd.tensor_tensor(factor[:], sess_sb[s][:], wgs_sb[t], ALU.mult)
             total = ring.tile([P, S], F32, name="total", bufs=3)
             if s < 2:
                 nc.vector.tensor_tensor(total[:], acc_a[:], gate[:], ALU.add)
@@ -242,7 +252,7 @@ def tile_list_manual_help_scores_kernel(
             nc.sync.dma_start(out[P * m : P * (m + 1), :], res[:])
 
         total = first_stage(0)
-        w4_scp.append(deal(w4_planes, 1, U8, "w4_scp1"))
+        w4_scp.append(deal(w4_planes[:, :, KP:H], U8, "w4_scp1"))
         for s in range(8):
             rewrite(s, total)
             if s + 1 < 8:

@@ -1,7 +1,6 @@
 from contextlib import ExitStack
 
 import concourse.mybir as mybir
-from concourse.masks import make_identity
 
 K, T, S, H, T2, NP, T3, S2 = 1024, 2048, 512, 1024, 1024, 512, 2048, 1024
 FLOPS = 2 * (2 * K * H * S + 2 * H * S2 * NP)
@@ -65,7 +64,7 @@ def tile_list_manual_help_scores_kernel(
                 )
 
         def load_w1(a, b):
-            dst = ring.tile([P, PACK, KP], F32, name="wide")
+            dst = held([P, PACK, KP], F32, "wide%d" % (2 * b + a))
             nc.sync.dma_start(dst[:], w1[KP * a : KP * (a + 1), KP * b : KP * (b + 1)].rearrange("(p i) c -> p i c", i=PACK))
             return dst
 
@@ -112,10 +111,10 @@ def tile_list_manual_help_scores_kernel(
         wgs_sb = load_wgs(0, 1)
         page = [load_rows(page0, 0, "page")]
         idx4 = load_list(offs4, NP, "idx4")
-        w1raw[(0, 1)] = load_w1(0, 1)
         sess_sb.append(load_rows(sess, 1, "sess"))
         wgs_sb = wgs_sb + load_wgs(1, PACK)
         page.append(load_rows(page0, 1, "page"))
+        w1raw[(0, 1)] = load_w1(0, 1)
         w1raw[(1, 1)] = load_w1(1, 1)
         for s in range(2, 8):
             sess_sb.append(load_rows(sess, s, "sess"))
@@ -127,8 +126,6 @@ def tile_list_manual_help_scores_kernel(
 
         v_w = [held([P, S], U32, "v_w%d" % a) for a in range(2)]
         v_sc = [held([P, S], U8, "v_sc%d" % a) for a in range(2)]
-        ident = held([P, P], F32, "ident")
-        make_identity(nc, ident[:])
 
         w1_q, w1_sc, v2_w = {}, {}, {}
 
@@ -168,9 +165,9 @@ def tile_list_manual_help_scores_kernel(
         prepare_w1(0, 0, "x_signed", w1_codes[:, 0, :])
         w4_planes = w4_sc[:].rearrange("p (a c) -> p a c", a=2)
         w4_scp = [deal(w4_planes[:, :, 0:KP], U8, "w4_scp0")]
-        v2_sc = held([P, S2], U8, "v2_sc")
+        prepare_w1(1, 0, "round10", w1_codes[:, 1, :])
+        v2_sc = held([P, S2], U8, "round10")
         nc.vector.tensor_copy(v2_sc[:], tab2_sc[:].indirect(idx2[:]))
-        prepare_w1(1, 0, "x_abs", w1_codes[:, 1, :])
 
         picked = {}
         x_q, x_sc = {}, {}
@@ -178,7 +175,7 @@ def tile_list_manual_help_scores_kernel(
         def first_stage(s):
             b, t = divmod(s, PACK)
             cols = slice(P * t, P * (t + 1))
-            acc_b, acc_a = bank(4 * (s % 2)), bank(4 * (s % 2) + 1)
+            acc_b, acc_a = bank(s % 2), bank(1 - s % 2)
             for a in range(2):
                 nc.tensor.matmul_mx(
                     acc_b[:], lhsT=w4_w[b][:, a, cols].bitcast(FP4X4), lhsT_scale=w4_scp[b][:, a, cols],
@@ -189,37 +186,25 @@ def tile_list_manual_help_scores_kernel(
                     acc_a[:], lhsT=w1_q[(a, b)][:, cols].bitcast(FP8X4), lhsT_scale=w1_sc[(a, b)][:, cols],
                     rhs=v_w[a][:].bitcast(FP8X4), rhs_scale=v_sc[a][:], start=(a == 0), stop=(a == 1),
                 )
-            gate = held([P, S], F32, "gate%d" % (s if s < 2 else 2 + s % 2))
+            gate = held([P, S], F32, "gate2" if s == 2 else ("wide1", "gate1")[s % 2])
             nc.scalar.activation(gate[:], acc_b[:], ACT.Tanh, bias=b4_col[:, b, t : t + 1])
-            factor = ring.tile([P, S], F32, name="factor", bufs=2)
-            nc.gpsimd.tensor_tensor(factor[:], sess_sb[s][:], wgs_sb[t], ALU.mult)
-            total = ring.tile([P, S], F32, name="total", bufs=3)
-            if s < 2:
-                nc.vector.tensor_tensor(total[:], acc_a[:], gate[:], ALU.add)
-                return total, factor
-            linear = ring.tile([P, S], F32, name="linear", bufs=2)
+            linear = held([P, S], F32, "linear%d" % (2 if s == 2 else s % 2))
             nc.scalar.copy(linear[:], acc_a[:])
-            sum_t = bank(2)
-            for c in range(4):
-                blk = slice(P * c, P * (c + 1))
-                nc.tensor.matmul(sum_t[:, blk], lhsT=gate[:, blk], rhs=ident[:], start=True, stop=False, is_transpose=True)
-                nc.tensor.matmul(sum_t[:, blk], lhsT=linear[:, blk], rhs=ident[:], start=False, stop=True, is_transpose=True)
-            turned = held([P, S], F32, "turned%d" % s)
-            nc.scalar.copy(turned[:], sum_t[:])
-            back = bank(3)
-            for c in range(4):
-                blk = slice(P * c, P * (c + 1))
-                nc.tensor.transpose(back[:, blk], turned[:, blk], ident[:])
-            nc.scalar.copy(total[:], back[:])
-            return total, factor
+            total = held([P, S], F32, "total")
+            nc.gpsimd.tensor_tensor(total[:], linear[:], gate[:], ALU.add)
+            factor = held([P, S], F32, ("factor", "linear2")[b])
+            nc.gpsimd.tensor_tensor(factor[:], sess_sb[s][:], wgs_sb[t], ALU.mult)
+            product = ring.tile([P, S], F32, name="product", bufs=2)
+            nc.gpsimd.tensor_tensor(product[:], total[:], factor[:], ALU.mult)
+            return product
 
-        def rewrite(s, total):
-            nc.vector.tensor_tensor(page[s][:].indirect(idx3[:]), total[0][:], total[1][:], ALU.mult)
+        def rewrite(s, product):
+            nc.vector.tensor_copy(page[s][:].indirect(idx3[:]), product[:])
 
         def pick(s):
             b, t = divmod(s, PACK)
             if t == 0:
-                picked[b] = ring.tile([P, PACK, NP], F32, name="wide")
+                picked[b] = held([P, PACK, NP], F32, "wide%d" % (2 * b))
             nc.vector.tensor_copy(picked[b][:, t, :], page[s][:].indirect(idx4[:]))
 
         def round_x(dst, b, n, t0, t1):
@@ -251,23 +236,23 @@ def tile_list_manual_help_scores_kernel(
             nc.vector.tensor_tensor(res[:], acc_e[:], res[:], ALU.max)
             nc.sync.dma_start(out[P * m : P * (m + 1), :], res[:])
 
-        total = first_stage(0)
+        products = {0: first_stage(0)}
         w4_scp.append(deal(w4_planes[:, :, KP:H], U8, "w4_scp1"))
         for s in range(8):
-            rewrite(s, total)
+            rewrite(s, products[s])
             if s + 1 < 8:
-                total = first_stage(s + 1)
+                products[s + 1] = first_stage(s + 1)
             pick(s)
             if s == 1:
                 w1_codes = held([P, 2, KP], U32, "page1")
-                prepare_w1(0, 1, "gate0", w1_codes[:, 0, :])
-                prepare_w1(1, 1, "gate1", w1_codes[:, 1, :])
+                prepare_w1(0, 1, "gate2", w1_codes[:, 0, :])
+                prepare_w1(1, 1, "linear2", w1_codes[:, 1, :])
             if s == 6:
-                first = [held([P, PACK * NP], BF16, "turned%d" % (5 + n)) for n in range(2)]
+                first = [held([P, PACK * NP], BF16, name) for name in ("wide1", "linear0")]
                 for n in range(2):
                     round_x(first[n], 0, n, 0, PACK)
                 quantize_x(0, 0, first[0], "page6")
-                second = [held([P, PACK * NP], BF16, name) for name in ("turned7", "turned5")]
+                second = [held([P, PACK * NP], BF16, name) for name in ("gate1", "linear1")]
                 for n in range(2):
                     round_x(second[n], 1, n, 0, 2)
         quantize_x(0, 1, first[1], "page7")
@@ -279,10 +264,10 @@ def tile_list_manual_help_scores_kernel(
                 score_pass(accs[m][n], m, n, 0)
         for n in range(2):
             round_x(second[n], 1, n, 2, PACK)
-        gather_v2(1, 0, "turned6")
+        gather_v2(1, 0, "linear0")
         quantize_x(1, 0, second[0], "x_signed")
-        gather_v2(1, 1, "turned7")
-        quantize_x(1, 1, second[1], "x_abs")
+        gather_v2(1, 1, "gate1")
+        quantize_x(1, 1, second[1], "wide3")
         for n in range(2):
             for m in range(4):
                 score_pass(accs[m][n], m, n, 1)

from contextlib import ExitStack

import concourse.mybir as mybir

K, T, S, H, T2, NP, T3, S2 = 1024, 2048, 512, 1024, 1024, 512, 2048, 1024
FLOPS = 2 * (2 * K * H * S + 2 * H * S2 * NP)

F32 = mybir.dt.float32
BF16 = mybir.dt.bfloat16
I32 = mybir.dt.int32
U32 = mybir.dt.uint32
U16 = mybir.dt.uint16
U8 = mybir.dt.uint8
FP8X4 = mybir.dt.float8_e4m3fn_x4
FP4X4 = mybir.dt.float4_e2m1fn_x4
ALU = mybir.AluOpType
ACT = mybir.ActivationFunctionType

P = 128
PACK = 4
KP = P * PACK


def tile_list_manual_help_scores_kernel(
    tc, tab_words, tab_scales, tab2_words, tab2_scales, w1, w4_words, w4_scales, b4, sess, wgs, page0, cv,
    offs, offs2, offs3, offs4, out,
):
    nc = tc.nc
    with ExitStack() as ctx:
        keep = ctx.enter_context(tc.tile_pool(name="keep", bufs=1))
        ring = ctx.enter_context(tc.tile_pool(name="ring", bufs=4))
        psum = ctx.enter_context(tc.psum_pool(name="psum", bufs=1))

        def held(shape, dtype, name):
            return keep.tile(shape, dtype, name=name, align_bytes=64)

        def bank(n):
            return psum.tile([P, 512], F32, name="bank%d" % n)

        def load_list(src, entries, name):
            dst = keep.tile([P, entries // 16], U16, name=name)
            nc.sync.dma_start(dst[:], src)
            return dst

        def load_words(src, a, name):
            dst = held([P, src.shape[2]], U32, name)
            nc.sync.dma_start(dst[:].bitcast(I32), src[a].rearrange("p t i -> p (t i)").bitcast(I32))
            return dst

        def zeroed_bytes(engine, width, name):
            dst = held([P, width], U8, name)
            engine.memset(dst[:].bitcast(I32), 0)
            return dst

        def load_scale_rows(queue, dst, src):
            for q in range(4):
                queue.dma_start(dst[32 * q : 32 * q + 8, :].bitcast(I32), src[:, 4 * q : 4 * q + 4, :].bitcast(I32))

        def load_scale_planes(queue, dst, src):
            for r in range(4):
                queue.dma_start(
                    dst[r:P:32, :].bitcast(I32).rearrange("q (a c) -> q a c", a=2),
                    src.bitcast(I32).rearrange("a (q r) c -> r q a c", r=4)[r],
                )

        def load_w1(a, b):
            dst = held([P, PACK, KP], F32, "wide%d" % (2 * b + a))
            nc.sync.dma_start(dst[:], w1[KP * a : KP * (a + 1), KP * b : KP * (b + 1)].rearrange("(p i) c -> p i c", i=PACK))
            return dst

        def load_w4(b):
            dst = held([P, 2, KP], U16, "w4raw%d" % b)
            nc.sync.dma_start(
                dst[:].bitcast(I32), w4_words[:, :, 2 * KP * b : 2 * KP * (b + 1)].rearrange("a p c -> p a c").bitcast(I32)
            )
            return dst

        def load_wgs(t0, t1):
            dst = held([P, t1 - t0, S], F32, "wgs%d" % t0)
            rows = wgs.rearrange("(q t) j -> q t j", t=PACK)[:, t0:t1, :]
            for q in range(4):
                nc.sync.dma_start(dst[32 * q : 32 * (q + 1), :, :], rows)
            return [dst[:, t, :] for t in range(t1 - t0)]

        def load_rows(src, s, name):
            b, t = divmod(s, PACK)
            dst = held([P, src.shape[1]], F32, "%s%d" % (name, s))
            nc.sync.dma_start(dst[:], src[KP * b : KP * (b + 1), :].rearrange("(p t) j -> t p j", t=PACK)[t])
            return dst

        tab_sc = zeroed_bytes(nc.vector, 2 * T, "tab_sc")
        w4_sc = zeroed_bytes(nc.vector, 2 * H, "w4_sc")
        tab2_sc = zeroed_bytes(nc.gpsimd, T3, "tab2_sc")

        w4raw = [load_w4(0)]
        idx = load_list(offs, S, "idx")
        tabw = [load_words(tab_words, 0, "tabw0")]
        w4raw.append(load_w4(1))
        idx2 = load_list(offs2, S2, "idx2")
        tab2w = [load_words(tab2_words, 0, "tab2w0")]
        w1raw = {(0, 0): load_w1(0, 0)}
        load_scale_planes(nc.gpsimd, tab_sc, tab_scales)
        load_scale_planes(nc.gpsimd, w4_sc, w4_scales)
        b4_col = held([P, 2, PACK], F32, "b4_col")
        nc.sync.dma_start(b4_col[:], b4.rearrange("(b p t) -> p b t", b=2, t=PACK))
        tabw.append(load_words(tab_words, 1, "tabw1"))
        load_scale_rows(nc.sync, tab2_sc, tab2_scales)
        w1raw[(1, 0)] = load_w1(1, 0)
        idx3 = load_list(offs3, S, "idx3")
        sess_sb = [load_rows(sess, 0, "sess")]
        wgs_sb = load_wgs(0, 1)
        page = [load_rows(page0, 0, "page")]
        idx4 = load_list(offs4, NP, "idx4")
        sess_sb.append(load_rows(sess, 1, "sess"))
        wgs_sb = wgs_sb + load_wgs(1, PACK)
        page.append(load_rows(page0, 1, "page"))
        w1raw[(0, 1)] = load_w1(0, 1)
        w1raw[(1, 1)] = load_w1(1, 1)
        for s in range(2, 8):
            sess_sb.append(load_rows(sess, s, "sess"))
            page.append(load_rows(page0, s, "page"))
        tab2w.append(load_words(tab2_words, 1, "tab2w1"))
        cv_col = held([P, S2 // P], F32, "cv_col")
        with nc.allow_non_contiguous_dma(reason="one factor a partition"):
            nc.sync.dma_start(cv_col[:], cv.rearrange("(c p) -> p c", p=P))

        v_w = [held([P, S], U32, "v_w%d" % a) for a in range(2)]
        v_sc = [held([P, S], U8, "v_sc%d" % a) for a in range(2)]

        w1_q, w1_sc, v2_w = {}, {}, {}

        def gather_v2(a, half, slot):
            v2_w[(a, half)] = held([P, S2 // 2], U32, slot)
            nc.vector.tensor_copy(v2_w[(a, half)][:], tab2w[a][:].indirect(idx2[:, 32 * half : 32 * (half + 1)]))

        def prepare_w1(a, b, slot, codes):
            rounded = held([P, PACK * KP], BF16, slot)
            nc.scalar.copy(
                rounded[:].rearrange("p (t m i) -> p m t i", t=PACK, i=PACK),
                w1raw[(a, b)][:].rearrange("p i (m t) -> p m t i", t=PACK),
            )
            w1_q[(a, b)] = codes
            w1_sc[(a, b)] = held([P, KP], U8, "w1_sc%d%d" % (a, b))
            nc.vector.quantize_mx(codes.bitcast(FP8X4), w1_sc[(a, b)][:], rounded[:])

        def deal(src, dtype, name):
            dst = held([P, 2, KP], dtype, name)
            nc.vector.tensor_copy(
                dst[:].rearrange("p a (t m) -> p a t m", t=PACK),
                src.rearrange("p a (m t) -> p a t m", t=PACK),
            )
            return dst

        w4_w = [deal(w4raw[0][:], U16, "w4_w0")]
        nc.vector.tensor_copy(v_w[0][:], tabw[0][:].indirect(idx[:]))
        w4_w.append(deal(w4raw[1][:], U16, "w4_w1"))
        v2_first = held([P, S2], U32, "v2_first")
        nc.vector.tensor_copy(v2_first[:], tab2w[0][:].indirect(idx2[:]))
        for half in range(2):
            v2_w[(0, half)] = v2_first[:, S2 // 2 * half : S2 // 2 * (half + 1)]
        for a in range(2):
            nc.vector.tensor_copy(v_sc[a][:], tab_sc[:, T * a : T * (a + 1)].indirect(idx[:]))
        nc.vector.tensor_copy(v_w[1][:], tabw[1][:].indirect(idx[:]))
        w1_codes = held([P, 2, KP], U32, "w1_codes")
        prepare_w1(0, 0, "x_signed", w1_codes[:, 0, :])
        w4_planes = w4_sc[:].rearrange("p (a c) -> p a c", a=2)
        w4_scp = [deal(w4_planes[:, :, 0:KP], U8, "w4_scp0")]
        prepare_w1(1, 0, "round10", w1_codes[:, 1, :])
        v2_sc = held([P, S2], U8, "round10")
        nc.vector.tensor_copy(v2_sc[:], tab2_sc[:].indirect(idx2[:]))

        picked = {}
        x_q, x_sc = {}, {}

        def first_stage(s):
            b, t = divmod(s, PACK)
            cols = slice(P * t, P * (t + 1))
            acc_b, acc_a = bank(s % 2), bank(1 - s % 2)
            for a in range(2):
                nc.tensor.matmul_mx(
                    acc_b[:], lhsT=w4_w[b][:, a, cols].bitcast(FP4X4), lhsT_scale=w4_scp[b][:, a, cols],
                    rhs=v_w[a][:].bitcast(FP8X4), rhs_scale=v_sc[a][:], start=(a == 0), stop=(a == 1),
                )
            for a in range(2):
                nc.tensor.matmul_mx(
                    acc_a[:], lhsT=w1_q[(a, b)][:, cols].bitcast(FP8X4), lhsT_scale=w1_sc[(a, b)][:, cols],
                    rhs=v_w[a][:].bitcast(FP8X4), rhs_scale=v_sc[a][:], start=(a == 0), stop=(a == 1),
                )
            gate = held([P, S], F32, "gate2" if s == 2 else ("wide1", "gate1")[s % 2])
            nc.scalar.activation(gate[:], acc_b[:], ACT.Tanh, bias=b4_col[:, b, t : t + 1])
            linear = held([P, S], F32, "linear%d" % (2 if s == 2 else s % 2))
            nc.scalar.copy(linear[:], acc_a[:])
            total = held([P, S], F32, "total")
            nc.gpsimd.tensor_tensor(total[:], linear[:], gate[:], ALU.add)
            factor = held([P, S], F32, ("factor", "linear2")[b])
            nc.gpsimd.tensor_tensor(factor[:], sess_sb[s][:], wgs_sb[t], ALU.mult)
            product = ring.tile([P, S], F32, name="product", bufs=2)
            nc.gpsimd.tensor_tensor(product[:], total[:], factor[:], ALU.mult)
            return product

        def rewrite(s, product):
            nc.vector.tensor_copy(page[s][:].indirect(idx3[:]), product[:])

        def pick(s):
            b, t = divmod(s, PACK)
            if t == 0:
                picked[b] = held([P, PACK, NP], F32, "wide%d" % (2 * b))
            nc.vector.tensor_copy(picked[b][:, t, :], page[s][:].indirect(idx4[:]))

        def round_x(dst, b, n, t0, t1):
            src = picked[b][:, t0:t1, :].rearrange("p t j -> p j t")
            view = dst[:].rearrange("p (j t) -> p j t", t=PACK)[:, :, t0:t1]
            if n == 0:
                nc.scalar.copy(view, src)
            else:
                nc.scalar.activation(view, src, ACT.Abs)

        def quantize_x(b, n, rounded, slot):
            x_q[(b, n)] = held([P, NP], U32, slot)
            x_sc[(b, n)] = held([P, NP], U8, "x_sc%d%d" % (b, n))
            nc.vector.quantize_mx(x_q[(b, n)][:].bitcast(FP8X4), x_sc[(b, n)][:], rounded[:])

        def score_pass(acc, m, n, b):
            half, c = divmod(m, 4)
            nc.tensor.matmul_mx(
                acc[:], lhsT=v2_w[(b, half)][:, P * c : P * (c + 1)].bitcast(FP8X4), lhsT_scale=v2_sc[4 * b : P, P * m : P * (m + 1)],
                rhs=x_q[(b, n)][:].bitcast(FP8X4), rhs_scale=x_sc[(b, n)][:], start=(b == 0), stop=(b == 1),
            )

        def scale_d(m, acc_d):
            res = ring.tile([P, NP], F32, name="res", bufs=8)
            nc.scalar.activation(res[:], acc_d[:], ACT.Copy, scale=cv_col[:, m : m + 1])
            return res

        def finish(m, res, acc_e):
            nc.vector.tensor_tensor(res[:], acc_e[:], res[:], ALU.max)
            nc.sync.dma_start(out[P * m : P * (m + 1), :], res[:])

        products = {0: first_stage(0)}
        w4_scp.append(deal(w4_planes[:, :, KP:H], U8, "w4_scp1"))
        for s in range(8):
            rewrite(s, products[s])
            if s + 1 < 8:
                products[s + 1] = first_stage(s + 1)
            pick(s)
            if s == 1:
                w1_codes = held([P, 2, KP], U32, "page1")
                prepare_w1(0, 1, "gate2", w1_codes[:, 0, :])
                prepare_w1(1, 1, "linear2", w1_codes[:, 1, :])
            if s == 6:
                first = [held([P, PACK * NP], BF16, name) for name in ("wide1", "linear0")]
                for n in range(2):
                    round_x(first[n], 0, n, 0, PACK)
                quantize_x(0, 0, first[0], "page6")
                second = [held([P, PACK * NP], BF16, name) for name in ("gate1", "linear1")]
                for n in range(2):
                    round_x(second[n], 1, n, 0, 2)
        quantize_x(0, 1, first[1], "page7")
        accs = {}
        for m in range(4):
            accs[m] = (bank((2 * m + 4) % 8), bank((2 * m + 5) % 8))
        for n in range(2):
            for m in range(4):
                score_pass(accs[m][n], m, n, 0)
        for n in range(2):
            round_x(second[n], 1, n, 2, PACK)
        gather_v2(1, 0, "linear0")
        quantize_x(1, 0, second[0], "x_signed")
        gather_v2(1, 1, "gate1")
        quantize_x(1, 1, second[1], "wide3")
        for n in range(2):
            for m in range(4):
                score_pass(accs[m][n], m, n, 1)

        def score_tile(m, n):
            acc = bank((2 * m + 4 + n) % 8)
            for b in range(2):
                score_pass(acc, m, n, b)
            return acc

        scaled = {m: scale_d(m, accs[m][0]) for m in range(4)}
        for m in range(4):
            finish(m, scaled[m], accs[m][1])
        scaled[4] = scale_d(4, score_tile(4, 0))
        for m in range(4, 8):
            if m + 1 < 8:
                scaled[m + 1] = scale_d(m + 1, score_tile(m + 1, 0))
            finish(m, scaled[m], score_tile(m, 1))
